import numpy as np
import ml_dtypes


def mxq(x, axis, fmt="e4m3"):
    dtype, down = {"e4m3": (ml_dtypes.float8_e4m3fn, 7), "e5m2": (ml_dtypes.float8_e5m2, 14)}[fmt]
    v = np.moveaxis(np.asarray(x, np.float32).astype(ml_dtypes.bfloat16).astype(np.float64), axis, -1)
    blocks = v.reshape(v.shape[:-1] + (-1, 32))
    amax = np.abs(blocks).max(-1, keepdims=True)
    byte = np.maximum(np.where(amax > 0, np.frexp(amax)[1] - 1 + 127, 0) - down, 1)
    scale = np.exp2(byte - 127.0)
    codes = (blocks / scale).astype(np.float32).astype(dtype).astype(np.float64)
    return np.moveaxis((codes * scale).reshape(v.shape), -1, axis)


WIDE = False


def mx_kscale(k):
    if not WIDE:
        return np.ones(k)
    levels = np.array([10, -10, 5, -5, 0])
    if k % 512:
        return np.exp2(np.random.permutation(np.resize(levels, k // 32))).repeat(32)
    a = np.empty((k // 512, 16))
    for p in range(k // 512):
        a[p, :8] = np.random.permutation(np.resize(levels, 8))
        for g in range(8):
            far = levels[np.abs(levels - a[p, g]) >= 10]
            a[p, g + 8] = far[np.random.randint(len(far))]
    return np.exp2(a.ravel()).repeat(32)


def f64(x):
    return np.asarray(x).astype(np.float64)


def striped(idx):
    return np.tile(idx.reshape(-1, 16).T, (8, 1)).astype(np.uint16)


def unstriped(offs):
    return offs[:16].T.reshape(-1).astype(np.int64)


E2M1 = np.array([0.0, 0.5, 1.0, 1.5, 2.0, 3.0, 4.0, 6.0, -0.0, -0.5, -1.0, -1.5, -2.0, -3.0, -4.0, -6.0])


def pack_weight(w, fmt):
    k, n = w.shape
    w = f64(np.asarray(w, np.float32).astype(ml_dtypes.bfloat16)).reshape(k // 32, 32, n)
    amax = np.abs(w).max(1)
    if fmt == "e4m3":
        byte = np.frexp(amax)[1] - 1 + 127 - 7
    else:
        mant, ex = np.frexp(amax / 6.0)
        byte = np.where(mant > 0.5, ex, ex - 1) + 127
    byte = np.clip(np.where(amax > 0, byte, 1), 1, 254)
    scaled = (w * np.exp2(127.0 - byte)[:, None, :]).reshape(k, n).astype(np.float32)
    by_word = np.ascontiguousarray(scaled.reshape(k // 512, 128, 4, n).transpose(0, 1, 3, 2))
    if fmt == "e4m3":
        words = by_word.astype(ml_dtypes.float8_e4m3fn).view(np.uint8)
    else:
        c = by_word.astype(ml_dtypes.float4_e2m1fn).view(np.uint8) & 0xF
        words = (c[..., 0::2] | (c[..., 1::2] << 4)).reshape(k // 512, 128, 2 * n)
    return np.ascontiguousarray(words), np.ascontiguousarray(byte.astype(np.uint8).reshape(k // 512, 16, n))


def unpack_weight(words, scales, fmt):
    g, _, n = scales.shape
    words = np.ascontiguousarray(words).reshape(g, 128, n, -1)
    if fmt == "e4m3":
        vals = words.view(ml_dtypes.float8_e4m3fn).astype(np.float64)
    else:
        nib = np.empty((g, 128, n, 4), np.uint8)
        nib[..., 0::2] = words & 0xF
        nib[..., 1::2] = words >> 4
        vals = E2M1[nib]
    vals = vals * np.repeat(np.exp2(scales.astype(np.float64) - 127.0), 8, axis=1)[..., None]
    return vals.transpose(0, 1, 3, 2).reshape(g * 512, n)


def d_relu2(v):
    return 2.0 * np.maximum(v, 0.0)


K, T, E, C, H, N = 128, 640, 5, 256, 512, 2048


def by_expert(wq, xq):
    return np.concatenate([wq[e].T @ xq[:, e * C:(e + 1) * C] for e in range(E)], axis=1)


def setup_inputs():
    n = np.random.standard_normal
    s = mx_kscale(N)[:, None]
    u = mx_kscale(H)
    first = np.random.permutation(np.repeat(np.arange(E), T // E))
    second = (first + 1 + np.random.permutation(np.repeat(np.arange(E - 1), -(-T // (E - 1)))[:T])) % E
    while np.bincount(second, minlength=E).max() != T // E:
        load = np.bincount(second, minlength=E); hi, lo = int(load.argmax()), int(load.argmin())
        t = np.flatnonzero((second == hi) & (first != lo))[0]; second[t] = lo
    slot_token = np.empty(E * C, np.int64); pos = np.empty((2, T), np.int64); fill = np.zeros(E, np.int64)
    place = np.stack([np.random.permutation(C) for _ in range(E)])
    for r, deal in enumerate((first, second)):
        for t in np.random.permutation(T):
            e = deal[t]; j = e * C + place[e, fill[e]]; fill[e] += 1; slot_token[j] = t; pos[r, t] = j
    g = np.random.uniform(0.2, 0.8, T)
    w_slot = np.empty(E * C); w_slot[pos[0]] = g; w_slot[pos[1]] = 1.0 - g
    dy = pack_weight(n((N, T)) * s, "e4m3")
    w2 = [pack_weight(m, "e2m1") for m in n((E, N, H)) / np.sqrt(N) / s[None] * u[None, None, :]]
    w1 = [pack_weight(m, "e2m1") for m in n((E, H, K)) / np.sqrt(H) / u[None, :, None]]
    return {
        "dy_words": dy[0],
        "dy_scales": dy[1],
        "a": n((H, E * C)).astype(np.float32),
        "w2_words": np.stack([m[0] for m in w2]),
        "w2_scales": np.stack([m[1] for m in w2]),
        "w1_words": np.stack([m[0] for m in w1]),
        "w1_scales": np.stack([m[1] for m in w1]),
        "gate": np.tile(w_slot, (H, 1)).astype(np.float32),
        "offs": striped(slot_token),
        "pos1": striped(pos[0]),
        "pos2": striped(pos[1]),
    }


def reference(dy_words, dy_scales, a, w2_words, w2_scales, w1_words, w1_scales, gate, offs, pos1, pos2):
    idx = unstriped(offs)
    w2 = np.stack([unpack_weight(w2_words[e], w2_scales[e], "e2m1") for e in range(E)])
    w1 = np.stack([unpack_weight(w1_words[e], w1_scales[e], "e2m1") for e in range(E)])
    gq = unpack_weight(dy_words, dy_scales, "e4m3")[:, idx]
    dh = f64(gate) * by_expert(w2, gq)
    da = dh * d_relu2(f64(a))
    dx = by_expert(w1, mxq(da, 0, "e4m3"))
    return dx[:, unstriped(pos1)] + dx[:, unstriped(pos2)]

@@ -1,0 +1,243 @@
+from contextlib import ExitStack
+
+import concourse.mybir as mybir
+from concourse.masks import make_identity
+
+K, T, E, C, H, N = 128, 640, 5, 256, 512, 2048
+S = E * C
+P = 128
+PASSES = N // 512
+TILES = S // P
+
+FLOPS = 2 * S * H * (N + K)
+BYTES = N * T + N * T // 32 + 4 * H * S + E * (N * H + H * K) * 17 // 32 + 4 * S + 2 * P * (S + 2 * T) // 16 + 4 * K * T
+
+F32 = mybir.dt.float32
+BF16 = mybir.dt.bfloat16
+I32 = mybir.dt.int32
+U32 = mybir.dt.uint32
+U16 = mybir.dt.uint16
+U8 = mybir.dt.uint8
+FP8X4 = mybir.dt.float8_e4m3fn_x4
+FP4X4 = mybir.dt.float4_e2m1fn_x4
+COPY = mybir.ActivationFunctionType.Copy
+RELU = mybir.ActivationFunctionType.Relu
+MULT = mybir.AluOpType.mult
+ADD = mybir.AluOpType.add
+
+SCALE_CUTS = (0, 448, 896, S)
+SHIFT_ROWS = 112
+W2_BYTES = PASSES * 2 * H
+EARLY = 2
+SUM_BANKS = 4
+TURN_BANKS = 4
+
+
+def tile_moe_bdx_mlp_relu2_kernel(
+    tc, dy_words, dy_scales, a, w2_words, w2_scales, w1_words, w1_scales, gate, offs, pos1, pos2, out
+):
+    nc = tc.nc
+    with ExitStack() as ctx:
+        lists = ctx.enter_context(tc.tile_pool(name="lists", bufs=1))
+        keep = ctx.enter_context(tc.tile_pool(name="keep", bufs=1))
+        psum = ctx.enter_context(tc.psum_pool(name="psum", bufs=1))
+
+        def zero(engine, tile_ap):
+            engine.memset(tile_ap.bitcast(I32), 0)
+
+        offs_sb = lists.tile([P, S // 16], U16, name="offs_sb")
+        pos1_sb = lists.tile([P, T // 16], U16, name="pos1_sb")
+        pos2_sb = lists.tile([P, T // 16], U16, name="pos2_sb")
+
+        token_scales = keep.tile([P, T], U8, name="token_scales", align_bytes=64)
+        w2_early = keep.tile([P, EARLY * PASSES * H], U8, name="w2_early", align_bytes=64)
+        w2_late = keep.tile([P, (E - EARLY) * PASSES * H], U8, name="w2_late", align_bytes=64)
+        w1_plane = keep.tile([P, E * K], U8, name="w1_plane", align_bytes=64)
+        slot_planes = keep.tile([P, (PASSES - 1) * S], U8, name="slot_planes", align_bytes=64)
+        gate_rows = keep.tile([P, P], F32, name="gate_rows")
+        identity = keep.tile([P, P], F32, name="identity")
+        zero(nc.gpsimd, token_scales[:])
+        zero(nc.gpsimd, w2_early[:])
+        zero(nc.vector, slot_planes[96:P, :])
+        zero(nc.vector, w1_plane[:])
+        nc.gpsimd.memset(gate_rows[0 : P - TILES, :], 0.0)
+        make_identity(nc, identity[:])
+        zero(nc.gpsimd, w2_late[:])
+
+        nc.sync.dma_start(offs_sb[:], offs)
+        nc.scalar.dma_start(gate_rows[P - TILES : P, :], gate[0:1, :].rearrange("o (c p) -> (o c) p", p=P))
+        for q in range(4):
+            nc.sync.dma_start(
+                token_scales[32 * q : 32 * q + 16, :].bitcast(I32),
+                dy_scales[:, 4 * q : 4 * q + 4, :].bitcast(I32),
+            )
+        words = keep.tile([P, PASSES * T], I32, name="token_words", align_bytes=64)
+        nc.sync.dma_start(
+            words[:].rearrange("p (o t) -> p o t", o=PASSES),
+            dy_words.rearrange("o p t d -> p o (t d)").bitcast(I32),
+        )
+        token_words = [words[:, o * T : (o + 1) * T].bitcast(U32) for o in range(PASSES)]
+
+        def load_plane(queue, plane, scales, groups):
+            for q in range(4):
+                queue.dma_start(
+                    plane[32 * q : 32 * q + 4, :].bitcast(I32).rearrange("r (g n) -> r g n", g=groups),
+                    scales.rearrange("e s (q r) n -> q r (e s) n", r=4)[q].bitcast(I32),
+                )
+
+        load_plane(nc.sync, w2_early, w2_scales[0:EARLY], EARLY * PASSES)
+
+        w2_sb, a_sb = [None] * E, [None] * E
+
+        def load_w2(first, count):
+            held = keep.tile([P, count * W2_BYTES], U8, name=f"w2_sb{first}", align_bytes=64)
+            nc.sync.dma_start(
+                held[:].bitcast(I32).rearrange("p (g n) -> p g n", g=count * PASSES),
+                w2_words[first : first + count].rearrange("e s p b -> p (e s) b").bitcast(I32),
+            )
+            for j in range(count):
+                w2_sb[first + j] = held[:, j * W2_BYTES : (j + 1) * W2_BYTES]
+
+        def load_a(e):
+            a_sb[e] = keep.tile([P, 4, C], F32, name=f"a_sb{e}", align_bytes=64)
+            nc.sync.dma_start(a_sb[e][:], a[:, e * C : (e + 1) * C].rearrange("(p t) s -> p t s", t=4))
+
+        load_w2(0, 1)
+
+        slot_scales = keep.tile([P, S], U8, name="slot_scales", align_bytes=64)
+        for lo, hi in zip(SCALE_CUTS, SCALE_CUTS[1:]):
+            nc.vector.tensor_copy(slot_scales[:, lo:hi], token_scales[:].indirect(offs_sb[:, lo // 16 : hi // 16]))
+        for o in range(1, PASSES):
+            nc.sync.dma_start(
+                slot_planes[0:SHIFT_ROWS, (o - 1) * S : o * S].bitcast(I32),
+                slot_scales[4 * o : 4 * o + SHIFT_ROWS, :].bitcast(I32),
+            )
+
+        load_w2(1, 1)
+        load_plane(nc.sync, w2_late, w2_scales[EARLY:E], (E - EARLY) * PASSES)
+        load_w2(2, 1)
+        load_w2(3, 1)
+        load_a(0)
+        load_w2(4, 1)
+        for e in range(1, E):
+            load_a(e)
+        w1_sb = keep.tile([P, E * 2 * K], U8, name="w1_sb", align_bytes=64)
+        nc.sync.dma_start(
+            w1_sb[:].bitcast(I32).rearrange("p (e n) -> p e n", e=E),
+            w1_words.rearrange("e o p b -> p (e o) b").bitcast(I32),
+        )
+        load_plane(nc.sync, w1_plane, w1_scales, E)
+        nc.sync.dma_start(pos1_sb[:], pos1)
+        nc.sync.dma_start(pos2_sb[:], pos2)
+
+        def slot_plane(o, n):
+            if o == 0:
+                return slot_scales[:, n * P : (n + 1) * P]
+            return slot_planes[:, (o - 1) * S + n * P : (o - 1) * S + (n + 1) * P]
+
+        def w2_plane(e, o):
+            held, g = (w2_early, e * PASSES + o) if e < EARLY else (w2_late, (e - EARLY) * PASSES + o)
+            return held[:, g * H : (g + 1) * H]
+
+        gate_ps = psum.tile([P, P], F32, name="gate_ps", tag=f"turn{TURN_BANKS - 1}")
+        nc.tensor.transpose(gate_ps[:], gate_rows[:], identity[:])
+        gate2 = keep.tile([P, TILES], F32, name="gate2")
+        nc.scalar.activation(gate2[:], gate_ps[:, P - TILES : P], COPY, scale=2.0)
+
+        slot_words, relu_a, gated, turned = [None] * E, [None] * E, [None] * TILES, [None] * TILES
+        da_codes, da_scales = [None] * E, [None] * E
+        dx = keep.tile([P, S], F32, name="dx")
+
+        def gather(e):
+            slot_words[e] = keep.tile([P, PASSES * C], U32, name=f"slot_words{e}", align_bytes=64)
+            for o in range(PASSES):
+                nc.vector.tensor_copy(
+                    slot_words[e][:, o * C : (o + 1) * C],
+                    token_words[o].indirect(offs_sb[:, e * C // 16 : (e + 1) * C // 16]),
+                )
+
+        def first_product(e):
+            sums = [psum.tile([P, H], F32, name=f"sums{n}", tag=f"sum{n % SUM_BANKS}") for n in (2 * e, 2 * e + 1)]
+            for o in range(PASSES):
+                for h in range(2):
+                    n = 2 * e + h
+                    nc.tensor.matmul_mx(
+                        out=sums[h][:],
+                        lhsT=slot_words[e][:, o * C + h * P : o * C + (h + 1) * P].bitcast(FP8X4),
+                        lhsT_scale=slot_plane(o, n),
+                        rhs=w2_sb[e][:, o * 2 * H : (o + 1) * 2 * H].bitcast(FP4X4),
+                        rhs_scale=w2_plane(e, o),
+                        start=(o == 0),
+                        stop=(o == PASSES - 1),
+                    )
+            for h in range(2):
+                n = 2 * e + h
+                gated[n] = keep.tile([P, 4, P], F32, name=f"gated{n}")
+                nc.scalar.activation(
+                    gated[n][:], sums[h][:].rearrange("s (p t) -> s t p", t=4), COPY, scale=gate2[:, n : n + 1]
+                )
+
+        def rectify(e):
+            relu_a[e] = keep.tile([P, C, 4], F32, name=f"relu_a{e}", align_bytes=64)
+            for h in range(2):
+                nc.scalar.activation(
+                    relu_a[e][:, h * P : (h + 1) * P, :],
+                    a_sb[e][:, :, h * P : (h + 1) * P].rearrange("p t s -> p s t"),
+                    RELU,
+                )
+
+        def turn(e):
+            for n in (2 * e, 2 * e + 1):
+                turned[n] = psum.tile([P, 4, P], F32, name=f"turned{n}", tag=f"turn{n % TURN_BANKS}")
+                for t in range(4):
+                    nc.tensor.transpose(turned[n][:, t, :], gated[n][:, t, :], identity[:])
+
+        def derive(e):
+            da = keep.tile([P, C, 4], BF16, name=f"da{e}", align_bytes=64)
+            for h in range(2):
+                nc.vector.tensor_tensor(
+                    da[:, h * P : (h + 1) * P, :],
+                    turned[2 * e + h][:].rearrange("p t s -> p s t"),
+                    relu_a[e][:, h * P : (h + 1) * P, :],
+                    MULT,
+                )
+            da_codes[e] = keep.tile([P, C], U32, name=f"da_codes{e}", align_bytes=64)
+            da_scales[e] = keep.tile([P, C], U8, name=f"da_scales{e}", align_bytes=64)
+            nc.vector.quantize_mx(
+                out=da_codes[e][:].bitcast(FP8X4), scales=da_scales[e][:], in_=da[:].rearrange("p s t -> p (s t)")
+            )
+
+        def second_product(e):
+            res = psum.tile([P, C], F32, name=f"res{e}", tag=f"sum{(TILES - 1 - e) % SUM_BANKS}")
+            nc.tensor.matmul_mx(
+                out=res[:],
+                lhsT=w1_sb[:, e * 2 * K : (e + 1) * 2 * K].bitcast(FP4X4),
+                lhsT_scale=w1_plane[:, e * K : (e + 1) * K],
+                rhs=da_codes[e][:].bitcast(FP8X4),
+                rhs_scale=da_scales[e][:],
+                start=True,
+                stop=True,
+            )
+            nc.scalar.copy(dx[:, e * C : (e + 1) * C], res[:])
+
+        for step in range(E + 3):
+            if step < E:
+                gather(step)
+            if 0 <= step - 1 < E:
+                first_product(step - 1)
+                rectify(step - 1)
+            if 0 <= step - 2 < E:
+                turn(step - 2)
+            if 0 <= step - 3 < E:
+                derive(step - 3)
+        for e in range(E):
+            second_product(e)
+
+        half = T // 2
+        for h in range(2):
+            first = keep.tile([P, half], F32, name=f"first{h}")
+            both = keep.tile([P, half], F32, name=f"both{h}")
+            cols = slice(h * half // 16, (h + 1) * half // 16)
+            nc.vector.tensor_copy(first[:], dx[:].indirect(pos1_sb[:, cols]))
+            nc.vector.tensor_tensor(both[:], dx[:].indirect(pos2_sb[:, cols]), first[:], ADD)
+            nc.sync.dma_start(out[:, h * half : (h + 1) * half], both[:])

@@ -29,8 +29,8 @@ SCALE_CUTS = (0, 448, 896, S)
 SHIFT_ROWS = 112
 W2_BYTES = PASSES * 2 * H
 EARLY = 2
-SUM_BANKS = 4
-TURN_BANKS = 4
+SUM_BANK = (0, 2, 0, 2, 0)
+TURN_BANK = (4, 6, 4, 6, 2)
 
 
 def tile_moe_bdx_mlp_relu2_kernel(
@@ -79,13 +79,12 @@ def tile_moe_bdx_mlp_relu2_kernel(
         token_words = [words[:, o * T : (o + 1) * T].bitcast(U32) for o in range(PASSES)]
 
         def load_plane(queue, plane, scales, groups):
-            for q in range(4):
+            for r in range(4):
                 queue.dma_start(
-                    plane[32 * q : 32 * q + 4, :].bitcast(I32).rearrange("r (g n) -> r g n", g=groups),
-                    scales.rearrange("e s (q r) n -> q r (e s) n", r=4)[q].bitcast(I32),
+                    plane[r:P:32, :].bitcast(I32).rearrange("q (g n) -> q g n", g=groups),
+                    scales.rearrange("e s (q r) n -> r q (e s) n", r=4)[r].bitcast(I32),
                 )
 
-        load_plane(nc.sync, w2_early, w2_scales[0:EARLY], EARLY * PASSES)
 
         w2_sb, a_sb = [None] * E, [None] * E
 
@@ -99,10 +98,12 @@ def tile_moe_bdx_mlp_relu2_kernel(
                 w2_sb[first + j] = held[:, j * W2_BYTES : (j + 1) * W2_BYTES]
 
         def load_a(e):
-            a_sb[e] = keep.tile([P, 4, C], F32, name=f"a_sb{e}", align_bytes=64)
+            a_sb[e] = keep.tile([P, 4, C], F32, name=f"a_sb{e}")
             nc.sync.dma_start(a_sb[e][:], a[:, e * C : (e + 1) * C].rearrange("(p t) s -> p t s", t=4))
 
+        load_plane(nc.sync, w2_early, w2_scales[0:EARLY], EARLY * PASSES)
         load_w2(0, 1)
+        load_w2(1, 1)
 
         slot_scales = keep.tile([P, S], U8, name="slot_scales", align_bytes=64)
         for lo, hi in zip(SCALE_CUTS, SCALE_CUTS[1:]):
@@ -113,14 +114,11 @@ def tile_moe_bdx_mlp_relu2_kernel(
                 slot_scales[4 * o : 4 * o + SHIFT_ROWS, :].bitcast(I32),
             )
 
-        load_w2(1, 1)
         load_plane(nc.sync, w2_late, w2_scales[EARLY:E], (E - EARLY) * PASSES)
-        load_w2(2, 1)
-        load_w2(3, 1)
-        load_a(0)
-        load_w2(4, 1)
-        for e in range(1, E):
+        for e in range(E):
             load_a(e)
+            if e + EARLY < E:
+                load_w2(e + EARLY, 1)
         w1_sb = keep.tile([P, E * 2 * K], U8, name="w1_sb", align_bytes=64)
         nc.sync.dma_start(
             w1_sb[:].bitcast(I32).rearrange("p (e n) -> p e n", e=E),
@@ -139,7 +137,7 @@ def tile_moe_bdx_mlp_relu2_kernel(
             held, g = (w2_early, e * PASSES + o) if e < EARLY else (w2_late, (e - EARLY) * PASSES + o)
             return held[:, g * H : (g + 1) * H]
 
-        gate_ps = psum.tile([P, P], F32, name="gate_ps", tag=f"turn{TURN_BANKS - 1}")
+        gate_ps = psum.tile([P, P], F32, name="gate_ps", tag="bank7")
         nc.tensor.transpose(gate_ps[:], gate_rows[:], identity[:])
         gate2 = keep.tile([P, TILES], F32, name="gate2")
         nc.scalar.activation(gate2[:], gate_ps[:, P - TILES : P], COPY, scale=2.0)
@@ -157,7 +155,7 @@ def tile_moe_bdx_mlp_relu2_kernel(
                 )
 
         def first_product(e):
-            sums = [psum.tile([P, H], F32, name=f"sums{n}", tag=f"sum{n % SUM_BANKS}") for n in (2 * e, 2 * e + 1)]
+            sums = [psum.tile([P, H], F32, name=f"sums{n}", tag=f"bank{SUM_BANK[e] + n % 2}") for n in (2 * e, 2 * e + 1)]
             for o in range(PASSES):
                 for h in range(2):
                     n = 2 * e + h
@@ -188,7 +186,7 @@ def tile_moe_bdx_mlp_relu2_kernel(
 
         def turn(e):
             for n in (2 * e, 2 * e + 1):
-                turned[n] = psum.tile([P, 4, P], F32, name=f"turned{n}", tag=f"turn{n % TURN_BANKS}")
+                turned[n] = psum.tile([P, 4, P], F32, name=f"turned{n}", tag=f"bank{TURN_BANK[e] + n % 2}")
                 for t in range(4):
                     nc.tensor.transpose(turned[n][:, t, :], gated[n][:, t, :], identity[:])
 
@@ -203,22 +201,29 @@ def tile_moe_bdx_mlp_relu2_kernel(
                 )
             da_codes[e] = keep.tile([P, C], U32, name=f"da_codes{e}", align_bytes=64)
             da_scales[e] = keep.tile([P, C], U8, name=f"da_scales{e}", align_bytes=64)
-            nc.vector.quantize_mx(
-                out=da_codes[e][:].bitcast(FP8X4), scales=da_scales[e][:], in_=da[:].rearrange("p s t -> p (s t)")
-            )
+            width = P if e == E - 1 else C
+            for lo in range(0, C, width):
+                nc.vector.quantize_mx(
+                    out=da_codes[e][:, lo : lo + width].bitcast(FP8X4),
+                    scales=da_scales[e][:, lo : lo + width],
+                    in_=da[:, lo : lo + width, :].rearrange("p s t -> p (s t)"),
+                )
 
-        def second_product(e):
-            res = psum.tile([P, C], F32, name=f"res{e}", tag=f"sum{(TILES - 1 - e) % SUM_BANKS}")
-            nc.tensor.matmul_mx(
-                out=res[:],
-                lhsT=w1_sb[:, e * 2 * K : (e + 1) * 2 * K].bitcast(FP4X4),
-                lhsT_scale=w1_plane[:, e * K : (e + 1) * K],
-                rhs=da_codes[e][:].bitcast(FP8X4),
-                rhs_scale=da_scales[e][:],
-                start=True,
-                stop=True,
-            )
-            nc.scalar.copy(dx[:, e * C : (e + 1) * C], res[:])
+        def second_product(lo, hi, bank):
+            res = psum.tile([P, hi - lo], F32, name=f"res{bank}", tag=f"bank{bank}")
+            for at in range(lo, hi, C):
+                e, width = at // C, min(C, hi - at)
+                cols = slice(at - e * C, at - e * C + width)
+                nc.tensor.matmul_mx(
+                    out=res[:, at - lo : at - lo + width],
+                    lhsT=w1_sb[:, e * 2 * K : (e + 1) * 2 * K].bitcast(FP4X4),
+                    lhsT_scale=w1_plane[:, e * K : (e + 1) * K],
+                    rhs=da_codes[e][:, cols].bitcast(FP8X4),
+                    rhs_scale=da_scales[e][:, cols],
+                    start=True,
+                    stop=True,
+                )
+            nc.scalar.copy(dx[:, lo:hi], res[:])
 
         for step in range(E + 3):
             if step < E:
@@ -230,8 +235,10 @@ def tile_moe_bdx_mlp_relu2_kernel(
                 turn(step - 2)
             if 0 <= step - 3 < E:
                 derive(step - 3)
-        for e in range(E):
-            second_product(e)
+        second_product(0, 2 * C, 0)
+        second_product(2 * C, 4 * C, 4)
+        second_product(4 * C, 4 * C + P, 5)
+        second_product(4 * C + P, S, 6)
 
         half = T // 2
         for h in range(2):

@@ -27,6 +27,8 @@ ADD = mybir.AluOpType.add
 
 SCALE_CUTS = (0, 448, 896, S)
 SHIFT_ROWS = 112
+SPARE = 64
+ON_GPSIMD = 1
 W2_BYTES = PASSES * 2 * H
 EARLY = 2
 SUM_BANK = (0, 2, 0, 2, 0)
@@ -71,12 +73,13 @@ def tile_moe_bdx_mlp_relu2_kernel(
                 token_scales[32 * q : 32 * q + 16, :].bitcast(I32),
                 dy_scales[:, 4 * q : 4 * q + 4, :].bitcast(I32),
             )
-        words = keep.tile([P, PASSES * T], I32, name="token_words", align_bytes=64)
+        words = keep.tile([P, PASSES * T + SPARE], I32, name="token_words", align_bytes=64)
+        nc.vector.memset(words[:, PASSES * T :], 0)
         nc.sync.dma_start(
-            words[:].rearrange("p (o t) -> p o t", o=PASSES),
+            words[:, 0 : PASSES * T].rearrange("p (o t) -> p o t", o=PASSES),
             dy_words.rearrange("o p t d -> p o (t d)").bitcast(I32),
         )
-        token_words = [words[:, o * T : (o + 1) * T].bitcast(U32) for o in range(PASSES)]
+        token_words = [words[:, o * T : (o + 1) * T + SPARE].bitcast(U32) for o in range(PASSES)]
 
         def load_plane(queue, plane, scales, groups):
             for r in range(4):
@@ -146,13 +149,16 @@ def tile_moe_bdx_mlp_relu2_kernel(
         da_codes, da_scales = [None] * E, [None] * E
         dx = keep.tile([P, S], F32, name="dx")
 
-        def gather(e):
-            slot_words[e] = keep.tile([P, PASSES * C], U32, name=f"slot_words{e}", align_bytes=64)
+        def gather(first, count):
+            width = count * C
+            held = keep.tile([P, PASSES * width], U32, name=f"slot_words{first}", align_bytes=64)
             for o in range(PASSES):
                 nc.vector.tensor_copy(
-                    slot_words[e][:, o * C : (o + 1) * C],
-                    token_words[o].indirect(offs_sb[:, e * C // 16 : (e + 1) * C // 16]),
+                    held[:, o * width : (o + 1) * width],
+                    token_words[o].indirect(offs_sb[:, first * C // 16 : (first * C + width) // 16]),
                 )
+            for j in range(count):
+                slot_words[first + j] = [held[:, o * width + j * C : o * width + (j + 1) * C] for o in range(PASSES)]
 
         def first_product(e):
             sums = [psum.tile([P, H], F32, name=f"sums{n}", tag=f"bank{SUM_BANK[e] + n % 2}") for n in (2 * e, 2 * e + 1)]
@@ -161,7 +167,7 @@ def tile_moe_bdx_mlp_relu2_kernel(
                     n = 2 * e + h
                     nc.tensor.matmul_mx(
                         out=sums[h][:],
-                        lhsT=slot_words[e][:, o * C + h * P : o * C + (h + 1) * P].bitcast(FP8X4),
+                        lhsT=slot_words[e][o][:, h * P : (h + 1) * P].bitcast(FP8X4),
                         lhsT_scale=slot_plane(o, n),
                         rhs=w2_sb[e][:, o * 2 * H : (o + 1) * 2 * H].bitcast(FP4X4),
                         rhs_scale=w2_plane(e, o),
@@ -193,12 +199,13 @@ def tile_moe_bdx_mlp_relu2_kernel(
         def derive(e):
             da = keep.tile([P, C, 4], BF16, name=f"da{e}", align_bytes=64)
             for h in range(2):
-                nc.vector.tensor_tensor(
-                    da[:, h * P : (h + 1) * P, :],
-                    turned[2 * e + h][:].rearrange("p t s -> p s t"),
-                    relu_a[e][:, h * P : (h + 1) * P, :],
-                    MULT,
-                )
+                dh = turned[2 * e + h][:].rearrange("p t s -> p s t")
+                engine = nc.vector
+                if e < ON_GPSIMD:
+                    staged = keep.tile([P, P, 4], F32, name=f"staged{2 * e + h}")
+                    nc.scalar.copy(staged[:], dh)
+                    dh, engine = staged[:], nc.gpsimd
+                engine.tensor_tensor(da[:, h * P : (h + 1) * P, :], dh, relu_a[e][:, h * P : (h + 1) * P, :], MULT)
             da_codes[e] = keep.tile([P, C], U32, name=f"da_codes{e}", align_bytes=64)
             da_scales[e] = keep.tile([P, C], U8, name=f"da_scales{e}", align_bytes=64)
             width = P if e == E - 1 else C
@@ -226,8 +233,8 @@ def tile_moe_bdx_mlp_relu2_kernel(
             nc.scalar.copy(dx[:, lo:hi], res[:])
 
         for step in range(E + 3):
-            if step < E:
-                gather(step)
+            if step < E and step % 2 == 0:
+                gather(step, min(2, E - step))
             if 0 <= step - 1 < E:
                 first_product(step - 1)
                 rectify(step - 1)

@@ -28,7 +28,6 @@ ADD = mybir.AluOpType.add
 SCALE_CUTS = (0, 448, 896, S)
 SHIFT_ROWS = 112
 SPARE = 64
-ON_GPSIMD = 1
 W2_BYTES = PASSES * 2 * H
 EARLY = 2
 SUM_BANK = (0, 2, 0, 2, 0)
@@ -185,8 +184,8 @@ def tile_moe_bdx_mlp_relu2_kernel(
             relu_a[e] = keep.tile([P, C, 4], F32, name=f"relu_a{e}", align_bytes=64)
             for h in range(2):
                 nc.scalar.activation(
-                    relu_a[e][:, h * P : (h + 1) * P, :],
-                    a_sb[e][:, :, h * P : (h + 1) * P].rearrange("p t s -> p s t"),
+                    relu_a[e][:, h * P : (h + 1) * P, :].rearrange("p (c i) t -> p c t i", i=4),
+                    a_sb[e][:, :, h * P : (h + 1) * P].rearrange("p t (c i) -> p c t i", i=4),
                     RELU,
                 )
 
@@ -199,13 +198,12 @@ def tile_moe_bdx_mlp_relu2_kernel(
         def derive(e):
             da = keep.tile([P, C, 4], BF16, name=f"da{e}", align_bytes=64)
             for h in range(2):
-                dh = turned[2 * e + h][:].rearrange("p t s -> p s t")
-                engine = nc.vector
-                if e < ON_GPSIMD:
-                    staged = keep.tile([P, P, 4], F32, name=f"staged{2 * e + h}")
-                    nc.scalar.copy(staged[:], dh)
-                    dh, engine = staged[:], nc.gpsimd
-                engine.tensor_tensor(da[:, h * P : (h + 1) * P, :], dh, relu_a[e][:, h * P : (h + 1) * P, :], MULT)
+                nc.vector.tensor_tensor(
+                    da[:, h * P : (h + 1) * P, :],
+                    turned[2 * e + h][:].rearrange("p t s -> p s t"),
+                    relu_a[e][:, h * P : (h + 1) * P, :],
+                    MULT,
+                )
             da_codes[e] = keep.tile([P, C], U32, name=f"da_codes{e}", align_bytes=64)
             da_scales[e] = keep.tile([P, C], U8, name=f"da_scales{e}", align_bytes=64)
             width = P if e == E - 1 else C

from contextlib import ExitStack

import concourse.mybir as mybir
from concourse.masks import make_identity

K, T, E, C, H, N = 128, 640, 5, 256, 512, 2048
S = E * C
P = 128
PASSES = N // 512
TILES = S // P

FLOPS = 2 * S * H * (N + K)
BYTES = N * T + N * T // 32 + 4 * H * S + E * (N * H + H * K) * 17 // 32 + 4 * S + 2 * P * (S + 2 * T) // 16 + 4 * K * T

F32 = mybir.dt.float32
BF16 = mybir.dt.bfloat16
I32 = mybir.dt.int32
U32 = mybir.dt.uint32
U16 = mybir.dt.uint16
U8 = mybir.dt.uint8
FP8X4 = mybir.dt.float8_e4m3fn_x4
FP4X4 = mybir.dt.float4_e2m1fn_x4
COPY = mybir.ActivationFunctionType.Copy
RELU = mybir.ActivationFunctionType.Relu
MULT = mybir.AluOpType.mult
ADD = mybir.AluOpType.add

SCALE_CUTS = (0, 448, 896, S)
SHIFT_ROWS = 112
SPARE = 64
W2_BYTES = PASSES * 2 * H
EARLY = 2
SUM_BANK = (0, 2, 0, 2, 0)
TURN_BANK = (4, 6, 4, 6, 2)


def tile_moe_bdx_mlp_relu2_kernel(
    tc, dy_words, dy_scales, a, w2_words, w2_scales, w1_words, w1_scales, gate, offs, pos1, pos2, out
):
    nc = tc.nc
    with ExitStack() as ctx:
        lists = ctx.enter_context(tc.tile_pool(name="lists", bufs=1))
        keep = ctx.enter_context(tc.tile_pool(name="keep", bufs=1))
        psum = ctx.enter_context(tc.psum_pool(name="psum", bufs=1))

        def zero(engine, tile_ap):
            engine.memset(tile_ap.bitcast(I32), 0)

        offs_sb = lists.tile([P, S // 16], U16, name="offs_sb")
        pos1_sb = lists.tile([P, T // 16], U16, name="pos1_sb")
        pos2_sb = lists.tile([P, T // 16], U16, name="pos2_sb")

        token_scales = keep.tile([P, T], U8, name="token_scales", align_bytes=64)
        w2_early = keep.tile([P, EARLY * PASSES * H], U8, name="w2_early", align_bytes=64)
        w2_late = keep.tile([P, (E - EARLY) * PASSES * H], U8, name="w2_late", align_bytes=64)
        w1_plane = keep.tile([P, E * K], U8, name="w1_plane", align_bytes=64)
        slot_planes = keep.tile([P, (PASSES - 1) * S], U8, name="slot_planes", align_bytes=64)
        gate_rows = keep.tile([P, P], F32, name="gate_rows")
        identity = keep.tile([P, P], F32, name="identity")
        zero(nc.gpsimd, token_scales[:])
        zero(nc.gpsimd, w2_early[:])
        zero(nc.vector, slot_planes[96:P, :])
        zero(nc.vector, w1_plane[:])
        nc.gpsimd.memset(gate_rows[0 : P - TILES, :], 0.0)
        make_identity(nc, identity[:])
        zero(nc.gpsimd, w2_late[:])

        nc.sync.dma_start(offs_sb[:], offs)
        nc.scalar.dma_start(gate_rows[P - TILES : P, :], gate[0:1, :].rearrange("o (c p) -> (o c) p", p=P))
        for q in range(4):
            nc.sync.dma_start(
                token_scales[32 * q : 32 * q + 16, :].bitcast(I32),
                dy_scales[:, 4 * q : 4 * q + 4, :].bitcast(I32),
            )
        words = keep.tile([P, PASSES * T + SPARE], I32, name="token_words", align_bytes=64)
        nc.vector.memset(words[:, PASSES * T :], 0)
        nc.sync.dma_start(
            words[:, 0 : PASSES * T].rearrange("p (o t) -> p o t", o=PASSES),
            dy_words.rearrange("o p t d -> p o (t d)").bitcast(I32),
        )
        token_words = [words[:, o * T : (o + 1) * T + SPARE].bitcast(U32) for o in range(PASSES)]

        def load_plane(queue, plane, scales, groups):
            for r in range(4):
                queue.dma_start(
                    plane[r:P:32, :].bitcast(I32).rearrange("q (g n) -> q g n", g=groups),
                    scales.rearrange("e s (q r) n -> r q (e s) n", r=4)[r].bitcast(I32),
                )


        w2_sb, a_sb = [None] * E, [None] * E

        def load_w2(first, count):
            held = keep.tile([P, count * W2_BYTES], U8, name=f"w2_sb{first}", align_bytes=64)
            nc.sync.dma_start(
                held[:].bitcast(I32).rearrange("p (g n) -> p g n", g=count * PASSES),
                w2_words[first : first + count].rearrange("e s p b -> p (e s) b").bitcast(I32),
            )
            for j in range(count):
                w2_sb[first + j] = held[:, j * W2_BYTES : (j + 1) * W2_BYTES]

        def load_a(e):
            a_sb[e] = keep.tile([P, 4, C], F32, name=f"a_sb{e}")
            nc.sync.dma_start(a_sb[e][:], a[:, e * C : (e + 1) * C].rearrange("(p t) s -> p t s", t=4))

        load_plane(nc.sync, w2_early, w2_scales[0:EARLY], EARLY * PASSES)
        load_w2(0, 1)
        load_w2(1, 1)

        slot_scales = keep.tile([P, S], U8, name="slot_scales", align_bytes=64)
        for lo, hi in zip(SCALE_CUTS, SCALE_CUTS[1:]):
            nc.vector.tensor_copy(slot_scales[:, lo:hi], token_scales[:].indirect(offs_sb[:, lo // 16 : hi // 16]))
        for o in range(1, PASSES):
            nc.sync.dma_start(
                slot_planes[0:SHIFT_ROWS, (o - 1) * S : o * S].bitcast(I32),
                slot_scales[4 * o : 4 * o + SHIFT_ROWS, :].bitcast(I32),
            )

        load_plane(nc.sync, w2_late, w2_scales[EARLY:E], (E - EARLY) * PASSES)
        for e in range(E):
            load_a(e)
            if e + EARLY < E:
                load_w2(e + EARLY, 1)
        w1_sb = keep.tile([P, E * 2 * K], U8, name="w1_sb", align_bytes=64)
        nc.sync.dma_start(
            w1_sb[:].bitcast(I32).rearrange("p (e n) -> p e n", e=E),
            w1_words.rearrange("e o p b -> p (e o) b").bitcast(I32),
        )
        load_plane(nc.sync, w1_plane, w1_scales, E)
        nc.sync.dma_start(pos1_sb[:], pos1)
        nc.sync.dma_start(pos2_sb[:], pos2)

        def slot_plane(o, n):
            if o == 0:
                return slot_scales[:, n * P : (n + 1) * P]
            return slot_planes[:, (o - 1) * S + n * P : (o - 1) * S + (n + 1) * P]

        def w2_plane(e, o):
            held, g = (w2_early, e * PASSES + o) if e < EARLY else (w2_late, (e - EARLY) * PASSES + o)
            return held[:, g * H : (g + 1) * H]

        gate_ps = psum.tile([P, P], F32, name="gate_ps", tag="bank7")
        nc.tensor.transpose(gate_ps[:], gate_rows[:], identity[:])
        gate2 = keep.tile([P, TILES], F32, name="gate2")
        nc.scalar.activation(gate2[:], gate_ps[:, P - TILES : P], COPY, scale=2.0)

        slot_words, relu_a, gated, turned = [None] * E, [None] * E, [None] * TILES, [None] * TILES
        da_codes, da_scales = [None] * E, [None] * E
        dx = keep.tile([P, S], F32, name="dx")

        def gather(first, count):
            width = count * C
            held = keep.tile([P, PASSES * width], U32, name=f"slot_words{first}", align_bytes=64)
            for o in range(PASSES):
                nc.vector.tensor_copy(
                    held[:, o * width : (o + 1) * width],
                    token_words[o].indirect(offs_sb[:, first * C // 16 : (first * C + width) // 16]),
                )
            for j in range(count):
                slot_words[first + j] = [held[:, o * width + j * C : o * width + (j + 1) * C] for o in range(PASSES)]

        def first_product(e):
            sums = [psum.tile([P, H], F32, name=f"sums{n}", tag=f"bank{SUM_BANK[e] + n % 2}") for n in (2 * e, 2 * e + 1)]
            for o in range(PASSES):
                for h in range(2):
                    n = 2 * e + h
                    nc.tensor.matmul_mx(
                        out=sums[h][:],
                        lhsT=slot_words[e][o][:, h * P : (h + 1) * P].bitcast(FP8X4),
                        lhsT_scale=slot_plane(o, n),
                        rhs=w2_sb[e][:, o * 2 * H : (o + 1) * 2 * H].bitcast(FP4X4),
                        rhs_scale=w2_plane(e, o),
                        start=(o == 0),
                        stop=(o == PASSES - 1),
                    )
            for h in range(2):
                n = 2 * e + h
                gated[n] = keep.tile([P, 4, P], F32, name=f"gated{n}")
                nc.scalar.activation(
                    gated[n][:], sums[h][:].rearrange("s (p t) -> s t p", t=4), COPY, scale=gate2[:, n : n + 1]
                )

        def rectify(e):
            relu_a[e] = keep.tile([P, C, 4], F32, name=f"relu_a{e}", align_bytes=64)
            for h in range(2):
                nc.scalar.activation(
                    relu_a[e][:, h * P : (h + 1) * P, :].rearrange("p (c i) t -> p c t i", i=4),
                    a_sb[e][:, :, h * P : (h + 1) * P].rearrange("p t (c i) -> p c t i", i=4),
                    RELU,
                )

        def turn(e):
            for n in (2 * e, 2 * e + 1):
                turned[n] = psum.tile([P, 4, P], F32, name=f"turned{n}", tag=f"bank{TURN_BANK[e] + n % 2}")
                for t in range(4):
                    nc.tensor.transpose(turned[n][:, t, :], gated[n][:, t, :], identity[:])

        def derive(e):
            da = keep.tile([P, C, 4], BF16, name=f"da{e}", align_bytes=64)
            for h in range(2):
                nc.vector.tensor_tensor(
                    da[:, h * P : (h + 1) * P, :],
                    turned[2 * e + h][:].rearrange("p t s -> p s t"),
                    relu_a[e][:, h * P : (h + 1) * P, :],
                    MULT,
                )
            da_codes[e] = keep.tile([P, C], U32, name=f"da_codes{e}", align_bytes=64)
            da_scales[e] = keep.tile([P, C], U8, name=f"da_scales{e}", align_bytes=64)
            width = P if e == E - 1 else C
            for lo in range(0, C, width):
                nc.vector.quantize_mx(
                    out=da_codes[e][:, lo : lo + width].bitcast(FP8X4),
                    scales=da_scales[e][:, lo : lo + width],
                    in_=da[:, lo : lo + width, :].rearrange("p s t -> p (s t)"),
                )

        def second_product(lo, hi, bank):
            res = psum.tile([P, hi - lo], F32, name=f"res{bank}", tag=f"bank{bank}")
            for at in range(lo, hi, C):
                e, width = at // C, min(C, hi - at)
                cols = slice(at - e * C, at - e * C + width)
                nc.tensor.matmul_mx(
                    out=res[:, at - lo : at - lo + width],
                    lhsT=w1_sb[:, e * 2 * K : (e + 1) * 2 * K].bitcast(FP4X4),
                    lhsT_scale=w1_plane[:, e * K : (e + 1) * K],
                    rhs=da_codes[e][:, cols].bitcast(FP8X4),
                    rhs_scale=da_scales[e][:, cols],
                    start=True,
                    stop=True,
                )
            nc.scalar.copy(dx[:, lo:hi], res[:])

        for step in range(E + 3):
            if step < E and step % 2 == 0:
                gather(step, min(2, E - step))
            if 0 <= step - 1 < E:
                first_product(step - 1)
                rectify(step - 1)
            if 0 <= step - 2 < E:
                turn(step - 2)
            if 0 <= step - 3 < E:
                derive(step - 3)
        second_product(0, 2 * C, 0)
        second_product(2 * C, 4 * C, 4)
        second_product(4 * C, 4 * C + P, 5)
        second_product(4 * C + P, S, 6)

        half = T // 2
        for h in range(2):
            first = keep.tile([P, half], F32, name=f"first{h}")
            both = keep.tile([P, half], F32, name=f"both{h}")
            cols = slice(h * half // 16, (h + 1) * half // 16)
            nc.vector.tensor_copy(first[:], dx[:].indirect(pos1_sb[:, cols]))
            nc.vector.tensor_tensor(both[:], dx[:].indirect(pos2_sb[:, cols]), first[:], ADD)
            nc.sync.dma_start(out[:, h * half : (h + 1) * half], both[:])
